import numpy as np
import ml_dtypes


def mxq(x, axis, fmt="e4m3"):
    dtype, down = {"e4m3": (ml_dtypes.float8_e4m3fn, 7), "e5m2": (ml_dtypes.float8_e5m2, 14)}[fmt]
    v = np.moveaxis(np.asarray(x, np.float32).astype(ml_dtypes.bfloat16).astype(np.float64), axis, -1)
    blocks = v.reshape(v.shape[:-1] + (-1, 32))
    amax = np.abs(blocks).max(-1, keepdims=True)
    byte = np.maximum(np.where(amax > 0, np.frexp(amax)[1] - 1 + 127, 0) - down, 1)
    scale = np.exp2(byte - 127.0)
    codes = (blocks / scale).astype(np.float32).astype(dtype).astype(np.float64)
    return np.moveaxis((codes * scale).reshape(v.shape), -1, axis)


WIDE = False


def mx_kscale(k):
    if not WIDE:
        return np.ones(k)
    levels = np.array([24, -24, 12, -12, 0])
    if k % 512:
        return np.exp2(np.random.permutation(np.resize(levels, k // 32))).repeat(32)
    a = np.empty((k // 512, 16))
    for p in range(k // 512):
        a[p, :8] = np.random.permutation(np.resize(levels, 8))
        for g in range(8):
            far = levels[np.abs(levels - a[p, g]) >= 10]
            a[p, g + 8] = far[np.random.randint(len(far))]
    return np.exp2(a.ravel()).repeat(32)


def f64(x):
    return np.asarray(x).astype(np.float64)


def striped8(idx):
    return np.concatenate([v.reshape(-1, 16).T for v in idx]).astype(np.uint16)


def unstriped8(offs):
    return np.stack([offs[16 * g:16 * g + 16].T.reshape(-1) for g in range(8)]).astype(np.int64)


E2M1 = np.array([0.0, 0.5, 1.0, 1.5, 2.0, 3.0, 4.0, 6.0, -0.0, -0.5, -1.0, -1.5, -2.0, -3.0, -4.0, -6.0])


def pack_weight(w, fmt):
    k, n = w.shape
    w = f64(np.asarray(w, np.float32).astype(ml_dtypes.bfloat16)).reshape(k // 32, 32, n)
    amax = np.abs(w).max(1)
    if fmt == "e4m3":
        byte = np.frexp(amax)[1] - 1 + 127 - 7
    else:
        mant, ex = np.frexp(amax / 6.0)
        byte = np.where(mant > 0.5, ex, ex - 1) + 127
    byte = np.clip(np.where(amax > 0, byte, 1), 1, 254)
    scaled = (w * np.exp2(127.0 - byte)[:, None, :]).reshape(k, n).astype(np.float32)
    by_word = np.ascontiguousarray(scaled.reshape(k // 512, 128, 4, n).transpose(0, 1, 3, 2))
    if fmt == "e4m3":
        words = by_word.astype(ml_dtypes.float8_e4m3fn).view(np.uint8)
    else:
        c = by_word.astype(ml_dtypes.float4_e2m1fn).view(np.uint8) & 0xF
        words = (c[..., 0::2] | (c[..., 1::2] << 4)).reshape(k // 512, 128, 2 * n)
    return np.ascontiguousarray(words), np.ascontiguousarray(byte.astype(np.uint8).reshape(k // 512, 16, n))


def unpack_weight(words, scales, fmt):
    g, _, n = scales.shape
    words = np.ascontiguousarray(words).reshape(g, 128, n, -1)
    if fmt == "e4m3":
        vals = words.view(ml_dtypes.float8_e4m3fn).astype(np.float64)
    else:
        nib = np.empty((g, 128, n, 4), np.uint8)
        nib[..., 0::2] = words & 0xF
        nib[..., 1::2] = words >> 4
        vals = E2M1[nib]
    vals = vals * np.repeat(np.exp2(scales.astype(np.float64) - 127.0), 8, axis=1)[..., None]
    return vals.transpose(0, 1, 3, 2).reshape(g * 512, n)


def silu(f):
    return f / (1.0 + np.exp(-np.maximum(f, -700.0)))


K, N, T, J = 512, 512, 2048, 512


def setup_inputs():
    n = np.random.standard_normal
    s = mx_kscale(K)[:, None]
    p_w = pack_weight(n((K, N)) / np.sqrt(K) / s, "e2m1")
    return {
        "xT": (n((K, T)) * s).astype(np.float32),
        "wgt": np.repeat(np.random.uniform(0.5, 2.0, (8, 3 * J)), 16, axis=0).astype(np.float32),
        "w_words": p_w[0],
        "w_scales": p_w[1],
        "b": (0.3 * n(N)).astype(np.float32),
        "offs": striped8(np.stack([np.concatenate([np.random.permutation(T)[:J] for _ in range(3)]) for _ in range(8)])),
    }


def reference(xT, wgt, w_words, w_scales, b, offs):
    idx = unstriped8(offs)
    rows = np.arange(K)
    xg = f64(wgt)[rows // 4 % 128] * f64(xT)[rows[:, None], idx[rows % 512 // 64]]
    xT_ = mxq(xg, 0, "e4m3").reshape(K, 3, J)
    w_ = unpack_weight(w_words, w_scales, "e2m1")
    a0 = w_.T @ xT_[:, 0]
    a1 = w_.T @ xT_[:, 1]
    a2 = w_.T @ xT_[:, 2]
    return silu(np.maximum(a0, 0.0) + np.maximum(a1, 0.0) + np.maximum(a2, 0.0) + f64(b)[:, None])

@@ -1,0 +1,139 @@
+from contextlib import ExitStack
+
+import concourse.mybir as mybir
+
+K, N, T, J, PICKS = 512, 512, 2048, 512, 3
+FLOPS = 2 * K * N * J * PICKS
+
+F32 = mybir.dt.float32
+BF16 = mybir.dt.bfloat16
+I32 = mybir.dt.int32
+U32 = mybir.dt.uint32
+U16 = mybir.dt.uint16
+U8 = mybir.dt.uint8
+FP8X4 = mybir.dt.float8_e4m3fn_x4
+FP4X4 = mybir.dt.float4_e2m1fn_x4
+ACT = mybir.ActivationFunctionType
+ALU = mybir.AluOpType
+
+P = 128
+PACK = 4
+STRIPE = 16
+HALF = 256
+NT = N // P
+
+
+def tile_list_relus_silu_kernel(tc, xT, wgt, w_words, w_scales, b, offs, out):
+    nc = tc.nc
+    with ExitStack() as ctx:
+        keep = ctx.enter_context(tc.tile_pool(name="keep", bufs=1))
+        psum = ctx.enter_context(tc.psum_pool(name="psum", bufs=1))
+
+        offsets = keep.tile([P, PICKS * J // STRIPE], U16, name="offsets")
+        planes = [keep.tile([P, T], F32, name=f"plane{i}") for i in range(PACK)]
+        weights = keep.tile([P, PICKS * J], F32, name="weights")
+        w_codes = keep.tile([P, 2 * N], U8, name="w_codes", align_bytes=64)
+        w_scale = keep.tile([P, N], U8, name="w_scale", align_bytes=64)
+        bias = keep.tile([P, NT], F32, name="bias")
+        seed = keep.tile([P, 8], F32, name="seed")
+        zero = keep.tile([P, 8], F32, name="zero")
+        banks = [psum.tile([P, 2, HALF], F32, name=f"bank{q}") for q in range(8)]
+
+        nc.vector.memset(seed[:], 0.0)
+        nc.vector.memset(w_scale[:].bitcast(U32), 0)
+        nc.scalar.activation(zero[:], seed[:], ACT.Silu)
+
+        x_planes = xT.rearrange("(p i) t -> i p t", i=PACK)
+        nc.sync.dma_start(offsets[:], offs)
+        nc.sync.dma_start(weights[:, 0:256], wgt[:, 0:256])
+        nc.sync.dma_start(planes[0][:], x_planes[0])
+        nc.sync.dma_start(weights[:, 256:768], wgt[:, 256:768])
+        nc.sync.dma_start(weights[:, 768:1536], wgt[:, 768:1536])
+        for i in range(1, PACK):
+            nc.sync.dma_start(planes[i][:], x_planes[i])
+        nc.sync.dma_start(w_codes[:].bitcast(I32), w_words[0].bitcast(I32))
+        for q in range(4):
+            nc.sync.dma_start(
+                w_scale[32 * q : 32 * q + 4, :].bitcast(I32), w_scales[0, 4 * q : 4 * q + 4, :].bitcast(I32)
+            )
+        with nc.allow_non_contiguous_dma(reason="one bias value a partition"):
+            nc.sync.dma_start(bias[:], b.rearrange("(t p) -> p t", p=P))
+
+        pieces = [(0, 0), (1, 0), (2, 0), (0, 1), (1, 1), (2, 1)]
+        rows = keep.tile([P, 18, HALF], F32, name="rows")
+        first_row = {(0, 0): 1, (1, 1): 0, (1, 0): 6, (2, 1): 5, (2, 0): 10, (0, 1): 14}
+        picked = {pc: rows[:, first_row[pc] : first_row[pc] + PACK, :] for pc in pieces}
+        bank_pair = {(0, 0): 0, (1, 0): 1, (2, 0): 2, (0, 1): 3, (1, 1): 0, (2, 1): 3}
+        pooled = [keep.tile([P, NT, HALF], F32, name=f"pooled{h}") for h in range(2)]
+        result = [keep.tile([P, NT, HALF], F32, name=f"result{h}") for h in range(2)]
+
+        def gather(i, pc):
+            first = pc[0] * J + pc[1] * HALF
+            nc.vector.tensor_tensor(
+                picked[pc][:, i, :],
+                planes[i][:].indirect(offsets[:, first // STRIPE : (first + HALF) // STRIPE]),
+                weights[:, first : first + HALF],
+                ALU.mult,
+            )
+
+        def project(pc):
+            name = f"{pc[0]}{pc[1]}"
+            grouped = keep.tile([P, HALF, PACK], BF16, name="grouped" + name, align_bytes=64)
+            codes = keep.tile([P, HALF], U32, name="codes" + name, align_bytes=64)
+            scales = keep.tile([P, HALF], U8, name="scales" + name, align_bytes=64)
+            nc.scalar.copy(
+                grouped[:].rearrange("p (c u) i -> p c i u", u=4),
+                picked[pc].rearrange("p i (c u) -> p c i u", u=4),
+            )
+            nc.vector.quantize_mx(
+                out=codes[:].bitcast(FP8X4), scales=scales[:], in_=grouped[:].rearrange("p j i -> p (j i)")
+            )
+            for nt in range(NT):
+                nc.tensor.matmul_mx(
+                    out=banks[2 * bank_pair[pc] + nt // 2][:, nt % 2, :],
+                    lhsT=w_codes[:, 2 * P * nt : 2 * P * (nt + 1)].bitcast(FP4X4),
+                    lhsT_scale=w_scale[:, P * nt : P * (nt + 1)],
+                    rhs=codes[:].bitcast(FP8X4),
+                    rhs_scale=scales[:],
+                    start=True,
+                    stop=True,
+                )
+            if pc[0] == 0:
+                for q in range(2):
+                    nc.scalar.activation(
+                        pooled[pc[1]][:, 2 * q : 2 * q + 2, :],
+                        banks[2 * bank_pair[pc] + q][:],
+                        ACT.Relu,
+                        bias=zero[:, 0:1],
+                    )
+
+        for pc in [(0, 0), (0, 1), (1, 0), (1, 1), (2, 0), (2, 1)]:
+            gather(0, pc)
+        for i in (1, 2):
+            for pc in pieces[:4]:
+                gather(i, pc)
+        for pc in pieces[:4]:
+            gather(3, pc)
+            project(pc)
+        for pc in pieces[4:]:
+            for i in (1, 2, 3):
+                gather(i, pc)
+            project(pc)
+
+        out_rows = out.rearrange("(t p) j -> p t j", p=P)
+        for h in range(2):
+            cols = slice(h * HALF, (h + 1) * HALF)
+            for c in (1, 2):
+                for q in range(2):
+                    part = pooled[h][:, 2 * q : 2 * q + 2, :]
+                    nc.vector.scalar_tensor_tensor(
+                        part, banks[2 * bank_pair[(c, h)] + q][:], 0.0, part, ALU.max, ALU.add
+                    )
+            for nt in range(NT):
+                nc.scalar.activation(
+                    result[h][:, nt, :], pooled[h][:, nt, :], ACT.Silu, bias=bias[:, nt : nt + 1]
+                )
+                if h == 1:
+                    nc.sync.dma_start(out_rows[:, nt, cols], result[h][:, nt, :])
+                elif nt % 2 == 1:
+                    nc.sync.dma_start(out_rows[:, nt - 1 : nt + 1, cols], result[h][:, nt - 1 : nt + 1, :])

@@ -1,6 +1,7 @@
 from contextlib import ExitStack
 
 import concourse.mybir as mybir
+from concourse.masks import make_identity
 
 K, N, T, J, PICKS = 512, 512, 2048, 512, 3
 FLOPS = 2 * K * N * J * PICKS
@@ -31,24 +32,27 @@ def tile_list_relus_silu_kernel(tc, xT, wgt, w_words, w_scales, b, offs, out):
 
         offsets = keep.tile([P, PICKS * J // STRIPE], U16, name="offsets")
         planes = [keep.tile([P, T], F32, name=f"plane{i}") for i in range(PACK)]
-        weights = keep.tile([P, PICKS * J], F32, name="weights")
+        rows = keep.tile([P, 26, HALF], F32, name="rows")
         w_codes = keep.tile([P, 2 * N], U8, name="w_codes", align_bytes=64)
         w_scale = keep.tile([P, N], U8, name="w_scale", align_bytes=64)
         bias = keep.tile([P, NT], F32, name="bias")
         seed = keep.tile([P, 8], F32, name="seed")
         zero = keep.tile([P, 8], F32, name="zero")
-        banks = [psum.tile([P, 2, HALF], F32, name=f"bank{q}") for q in range(8)]
+        ident = keep.tile([P, P], F32, name="ident")
+        banks = [psum.tile([P, 2 * HALF], F32, name=f"bank{q}") for q in range(8)]
 
         nc.vector.memset(seed[:], 0.0)
         nc.vector.memset(w_scale[:].bitcast(U32), 0)
         nc.scalar.activation(zero[:], seed[:], ACT.Silu)
+        make_identity(nc, ident[:])
 
         x_planes = xT.rearrange("(p i) t -> i p t", i=PACK)
+        wgt_rows = wgt.rearrange("p (r j) -> p r j", j=HALF)
         nc.sync.dma_start(offsets[:], offs)
-        nc.sync.dma_start(weights[:, 0:256], wgt[:, 0:256])
+        nc.sync.dma_start(rows[:, 0:1, :], wgt_rows[:, 0:1, :])
         nc.sync.dma_start(planes[0][:], x_planes[0])
-        nc.sync.dma_start(weights[:, 256:768], wgt[:, 256:768])
-        nc.sync.dma_start(weights[:, 768:1536], wgt[:, 768:1536])
+        nc.sync.dma_start(rows[:, 1:3, :], wgt_rows[:, 1:3, :])
+        nc.sync.dma_start(rows[:, 3:6, :], wgt_rows[:, 3:6, :])
         for i in range(1, PACK):
             nc.sync.dma_start(planes[i][:], x_planes[i])
         nc.sync.dma_start(w_codes[:].bitcast(I32), w_words[0].bitcast(I32))
@@ -60,80 +64,124 @@ def tile_list_relus_silu_kernel(tc, xT, wgt, w_words, w_scales, b, offs, out):
             nc.sync.dma_start(bias[:], b.rearrange("(t p) -> p t", p=P))
 
         pieces = [(0, 0), (1, 0), (2, 0), (0, 1), (1, 1), (2, 1)]
-        rows = keep.tile([P, 18, HALF], F32, name="rows")
-        first_row = {(0, 0): 1, (1, 1): 0, (1, 0): 6, (2, 1): 5, (2, 0): 10, (0, 1): 14}
-        picked = {pc: rows[:, first_row[pc] : first_row[pc] + PACK, :] for pc in pieces}
-        bank_pair = {(0, 0): 0, (1, 0): 1, (2, 0): 2, (0, 1): 3, (1, 1): 0, (2, 1): 3}
-        pooled = [keep.tile([P, NT, HALF], F32, name=f"pooled{h}") for h in range(2)]
+        weight_row = {pc: 2 * pc[0] + pc[1] for pc in pieces}
+        picked_row = {}
+        free_row = 6
+        for s, pc in enumerate(pieces):
+            for i in range(PACK):
+                if i == 2 and s >= 2:
+                    picked_row[pc, i] = weight_row[pieces[s - 2]]
+                else:
+                    picked_row[pc, i] = free_row
+                    free_row += 1
+        bank_pair = {(0, 0): 0, (1, 0): 1, (2, 0): 3, (0, 1): 0, (1, 1): 1, (2, 1): 3}
+        sum_pair = 2
+        grouped = {pc: keep.tile([P, HALF, PACK], BF16, name=f"grouped{pc[0]}{pc[1]}", align_bytes=64) for pc in pieces}
+        relus = [keep.tile([P, 2, N], F32, name=f"relus{c}") for c in range(PICKS)]
+        pooled = keep.tile([P, NT, HALF], F32, name="pooled")
         result = [keep.tile([P, NT, HALF], F32, name=f"result{h}") for h in range(2)]
+        out_rows = out.rearrange("(t p) j -> p t j", p=P)
 
         def gather(i, pc):
             first = pc[0] * J + pc[1] * HALF
             nc.vector.tensor_tensor(
-                picked[pc][:, i, :],
+                rows[:, picked_row[pc, i], :],
                 planes[i][:].indirect(offsets[:, first // STRIPE : (first + HALF) // STRIPE]),
-                weights[:, first : first + HALF],
+                rows[:, weight_row[pc], :],
                 ALU.mult,
             )
 
+        def round_pair(copy, pc, i):
+            r0, r1 = picked_row[pc, i], picked_row[pc, i + 1]
+            copy(grouped[pc][:, :, i : i + 2], rows[:, r0 : r1 + 1 : r1 - r0, :].rearrange("p i j -> p j i"))
+
         def project(pc):
             name = f"{pc[0]}{pc[1]}"
-            grouped = keep.tile([P, HALF, PACK], BF16, name="grouped" + name, align_bytes=64)
             codes = keep.tile([P, HALF], U32, name="codes" + name, align_bytes=64)
             scales = keep.tile([P, HALF], U8, name="scales" + name, align_bytes=64)
-            nc.scalar.copy(
-                grouped[:].rearrange("p (c u) i -> p c i u", u=4),
-                picked[pc].rearrange("p i (c u) -> p c i u", u=4),
-            )
             nc.vector.quantize_mx(
-                out=codes[:].bitcast(FP8X4), scales=scales[:], in_=grouped[:].rearrange("p j i -> p (j i)")
+                out=codes[:].bitcast(FP8X4), scales=scales[:], in_=grouped[pc][:].rearrange("p j i -> p (j i)")
             )
-            for nt in range(NT):
-                nc.tensor.matmul_mx(
-                    out=banks[2 * bank_pair[pc] + nt // 2][:, nt % 2, :],
-                    lhsT=w_codes[:, 2 * P * nt : 2 * P * (nt + 1)].bitcast(FP4X4),
-                    lhsT_scale=w_scale[:, P * nt : P * (nt + 1)],
-                    rhs=codes[:].bitcast(FP8X4),
-                    rhs_scale=scales[:],
-                    start=True,
-                    stop=True,
-                )
-            if pc[0] == 0:
-                for q in range(2):
-                    nc.scalar.activation(
-                        pooled[pc[1]][:, 2 * q : 2 * q + 2, :],
-                        banks[2 * bank_pair[pc] + q][:],
-                        ACT.Relu,
-                        bias=zero[:, 0:1],
+            pair = banks[2 * bank_pair[pc] : 2 * bank_pair[pc] + 2]
+            if pc[1] == 0:
+                for jt in range(2):
+                    nc.tensor.matmul_mx(
+                        out=pair[jt][:],
+                        lhsT=codes[:, P * jt : P * (jt + 1)].bitcast(FP8X4),
+                        lhsT_scale=scales[:, P * jt : P * (jt + 1)],
+                        rhs=w_codes[:].bitcast(FP4X4),
+                        rhs_scale=w_scale[:],
+                        start=True,
+                        stop=True,
+                    )
+            else:
+                for nt in range(NT):
+                    nc.tensor.matmul_mx(
+                        out=pair[nt // 2][:, HALF * (nt % 2) : HALF * (nt % 2 + 1)],
+                        lhsT=w_codes[:, 2 * P * nt : 2 * P * (nt + 1)].bitcast(FP4X4),
+                        lhsT_scale=w_scale[:, P * nt : P * (nt + 1)],
+                        rhs=codes[:].bitcast(FP8X4),
+                        rhs_scale=scales[:],
+                        start=True,
+                        stop=True,
                     )
 
-        for pc in [(0, 0), (0, 1), (1, 0), (1, 1), (2, 0), (2, 1)]:
-            gather(0, pc)
-        for i in (1, 2):
-            for pc in pieces[:4]:
-                gather(i, pc)
-        for pc in pieces[:4]:
-            gather(3, pc)
-            project(pc)
-        for pc in pieces[4:]:
-            for i in (1, 2, 3):
-                gather(i, pc)
-            project(pc)
+        def relu_first_half(c):
+            for jt in range(2):
+                nc.scalar.activation(relus[c][:, jt, :], banks[2 * bank_pair[c, 0] + jt][:], ACT.Relu, bias=zero[:, 0:1])
 
-        out_rows = out.rearrange("(t p) j -> p t j", p=P)
-        for h in range(2):
+        def turn_and_add(c):
+            for jt in range(2):
+                for nt in range(NT):
+                    col = HALF * (nt % 2) + P * jt
+                    nc.tensor.matmul(
+                        banks[2 * sum_pair + nt // 2][:, col : col + P],
+                        relus[c][:, jt, P * nt : P * (nt + 1)],
+                        ident[:],
+                        start=(c == 0 and col == 0),
+                        stop=(c == PICKS - 1 and col == 2 * HALF - P),
+                        is_transpose=True,
+                    )
+
+        def finish(h, nt, source):
+            nc.scalar.activation(result[h][:, nt, :], source, ACT.Silu, bias=bias[:, nt : nt + 1])
             cols = slice(h * HALF, (h + 1) * HALF)
-            for c in (1, 2):
-                for q in range(2):
-                    part = pooled[h][:, 2 * q : 2 * q + 2, :]
-                    nc.vector.scalar_tensor_tensor(
-                        part, banks[2 * bank_pair[(c, h)] + q][:], 0.0, part, ALU.max, ALU.add
-                    )
-            for nt in range(NT):
-                nc.scalar.activation(
-                    result[h][:, nt, :], pooled[h][:, nt, :], ACT.Silu, bias=bias[:, nt : nt + 1]
-                )
-                if h == 1:
-                    nc.sync.dma_start(out_rows[:, nt, cols], result[h][:, nt, :])
-                elif nt % 2 == 1:
-                    nc.sync.dma_start(out_rows[:, nt - 1 : nt + 1, cols], result[h][:, nt - 1 : nt + 1, :])
+            if h == 1 and nt >= 2:
+                nc.sync.dma_start(out_rows[:, nt, cols], result[h][:, nt, :])
+            elif nt % 2 == 1:
+                nc.sync.dma_start(out_rows[:, nt - 1 : nt + 1, cols], result[h][:, nt - 1 : nt + 1, :])
+
+        for pc in sorted(pieces):
+            gather(0, pc)
+        for pc in pieces:
+            gather(1, pc)
+            round_pair(nc.scalar.copy, pc, 0)
+        for pc in pieces[:2]:
+            gather(2, pc)
+        for s, pc in enumerate(pieces):
+            if s >= 2:
+                gather(2, pc)
+            gather(3, pc)
+            round_pair(nc.scalar.copy if s < 4 else nc.vector.tensor_copy, pc, 2)
+            if 2 <= s < 5:
+                relu_first_half(s - 2)
+            project(pc)
+            if 2 <= s < 5:
+                turn_and_add(s - 2)
+        for q in range(2):
+            nc.scalar.activation(
+                pooled[:, 2 * q : 2 * q + 2, :].rearrange("p t j -> p (t j)"),
+                banks[2 * bank_pair[0, 1] + q][:],
+                ACT.Relu,
+                bias=zero[:, 0:1],
+            )
+        for nt in range(NT):
+            finish(0, nt, banks[2 * sum_pair + nt // 2][:, HALF * (nt % 2) : HALF * (nt % 2 + 1)])
+        for q in range(2):
+            part = pooled[:, 2 * q : 2 * q + 2, :].rearrange("p t j -> p (t j)")
+            nc.vector.scalar_tensor_tensor(part, banks[2 * bank_pair[1, 1] + q][:], 0.0, part, ALU.max, ALU.add)
+        for nt in range(NT):
+            part = pooled[:, nt, :]
+            source = banks[2 * bank_pair[2, 1] + nt // 2][:, HALF * (nt % 2) : HALF * (nt % 2 + 1)]
+            nc.vector.scalar_tensor_tensor(part, source, 0.0, part, ALU.max, ALU.add)
+            finish(1, nt, part)

@@ -32,7 +32,7 @@ def tile_list_relus_silu_kernel(tc, xT, wgt, w_words, w_scales, b, offs, out):
 
         offsets = keep.tile([P, PICKS * J // STRIPE], U16, name="offsets")
         planes = [keep.tile([P, T], F32, name=f"plane{i}") for i in range(PACK)]
-        rows = keep.tile([P, 26, HALF], F32, name="rows")
+        strip = keep.tile([P, 26, HALF], F32, name="strip")
         w_codes = keep.tile([P, 2 * N], U8, name="w_codes", align_bytes=64)
         w_scale = keep.tile([P, N], U8, name="w_scale", align_bytes=64)
         bias = keep.tile([P, NT], F32, name="bias")
@@ -47,12 +47,11 @@ def tile_list_relus_silu_kernel(tc, xT, wgt, w_words, w_scales, b, offs, out):
         make_identity(nc, ident[:])
 
         x_planes = xT.rearrange("(p i) t -> i p t", i=PACK)
-        wgt_rows = wgt.rearrange("p (r j) -> p r j", j=HALF)
-        nc.sync.dma_start(offsets[:], offs)
-        nc.sync.dma_start(rows[:, 0:1, :], wgt_rows[:, 0:1, :])
+        flat = strip[:].rearrange("p s j -> p (s j)")
         nc.sync.dma_start(planes[0][:], x_planes[0])
-        nc.sync.dma_start(rows[:, 1:3, :], wgt_rows[:, 1:3, :])
-        nc.sync.dma_start(rows[:, 3:6, :], wgt_rows[:, 3:6, :])
+        nc.sync.dma_start(offsets[:], offs)
+        for lo, hi in ((0, 256), (256, 768), (768, 1536)):
+            nc.sync.dma_start(flat[:, lo:hi], wgt[:, lo:hi])
         for i in range(1, PACK):
             nc.sync.dma_start(planes[i][:], x_planes[i])
         nc.sync.dma_start(w_codes[:].bitcast(I32), w_words[0].bitcast(I32))
@@ -63,44 +62,38 @@ def tile_list_relus_silu_kernel(tc, xT, wgt, w_words, w_scales, b, offs, out):
         with nc.allow_non_contiguous_dma(reason="one bias value a partition"):
             nc.sync.dma_start(bias[:], b.rearrange("(t p) -> p t", p=P))
 
-        pieces = [(0, 0), (1, 0), (2, 0), (0, 1), (1, 1), (2, 1)]
-        weight_row = {pc: 2 * pc[0] + pc[1] for pc in pieces}
-        picked_row = {}
-        free_row = 6
-        for s, pc in enumerate(pieces):
-            for i in range(PACK):
-                if i == 2 and s >= 2:
-                    picked_row[pc, i] = weight_row[pieces[s - 2]]
-                else:
-                    picked_row[pc, i] = free_row
-                    free_row += 1
+        row = {0: range(14, 20), 1: range(20, 26), 2: (6, 2, 7, 4, 0, 1), 3: range(8, 14)}
         bank_pair = {(0, 0): 0, (1, 0): 1, (2, 0): 3, (0, 1): 0, (1, 1): 1, (2, 1): 3}
         sum_pair = 2
-        grouped = {pc: keep.tile([P, HALF, PACK], BF16, name=f"grouped{pc[0]}{pc[1]}", align_bytes=64) for pc in pieces}
+        grouped = keep.tile([P, PICKS * J, PACK], BF16, name="grouped", align_bytes=64)
         relus = [keep.tile([P, 2, N], F32, name=f"relus{c}") for c in range(PICKS)]
         pooled = keep.tile([P, NT, HALF], F32, name="pooled")
         result = [keep.tile([P, NT, HALF], F32, name=f"result{h}") for h in range(2)]
         out_rows = out.rearrange("(t p) j -> p t j", p=P)
 
-        def gather(i, pc):
-            first = pc[0] * J + pc[1] * HALF
+        def gather(i, lo, hi):
+            first = row[i][lo // HALF] * HALF
             nc.vector.tensor_tensor(
-                rows[:, picked_row[pc, i], :],
-                planes[i][:].indirect(offsets[:, first // STRIPE : (first + HALF) // STRIPE]),
-                rows[:, weight_row[pc], :],
+                flat[:, first : first + hi - lo],
+                planes[i][:].indirect(offsets[:, lo // STRIPE : hi // STRIPE]),
+                flat[:, lo:hi],
                 ALU.mult,
             )
 
-        def round_pair(copy, pc, i):
-            r0, r1 = picked_row[pc, i], picked_row[pc, i + 1]
-            copy(grouped[pc][:, :, i : i + 2], rows[:, r0 : r1 + 1 : r1 - r0, :].rearrange("p i j -> p j i"))
+        def round_pair(copy, i, lo, hi):
+            r0, r1 = row[i][lo // HALF], row[i + 1][lo // HALF]
+            both = strip[:, r0 : r1 + 1 : r1 - r0, :]
+            copy(grouped[:, lo:hi, i : i + 2], both.rearrange("p i j -> p j i"))
+
+        def span(pc):
+            return pc[0] * J + pc[1] * HALF, pc[0] * J + (pc[1] + 1) * HALF
 
         def project(pc):
             name = f"{pc[0]}{pc[1]}"
             codes = keep.tile([P, HALF], U32, name="codes" + name, align_bytes=64)
             scales = keep.tile([P, HALF], U8, name="scales" + name, align_bytes=64)
             nc.vector.quantize_mx(
-                out=codes[:].bitcast(FP8X4), scales=scales[:], in_=grouped[pc][:].rearrange("p j i -> p (j i)")
+                out=codes[:].bitcast(FP8X4), scales=scales[:], in_=grouped[:, span(pc)[0] : span(pc)[1], :].rearrange("p j i -> p (j i)")
             )
             pair = banks[2 * bank_pair[pc] : 2 * bank_pair[pc] + 2]
             if pc[1] == 0:
@@ -146,35 +139,45 @@ def tile_list_relus_silu_kernel(tc, xT, wgt, w_words, w_scales, b, offs, out):
         def finish(h, nt, source):
             nc.scalar.activation(result[h][:, nt, :], source, ACT.Silu, bias=bias[:, nt : nt + 1])
             cols = slice(h * HALF, (h + 1) * HALF)
-            if h == 1 and nt >= 2:
+            if h == 1 and nt == 3:
+                nc.scalar.dma_start(out_rows[:, nt, cols], result[h][:, nt, :])
+            elif h == 1 and nt == 2:
                 nc.sync.dma_start(out_rows[:, nt, cols], result[h][:, nt, :])
             elif nt % 2 == 1:
                 nc.sync.dma_start(out_rows[:, nt - 1 : nt + 1, cols], result[h][:, nt - 1 : nt + 1, :])
 
-        for pc in sorted(pieces):
-            gather(0, pc)
+        def relu_second_half():
+            for q in range(2):
+                nc.scalar.activation(
+                    pooled[:, 2 * q : 2 * q + 2, :].rearrange("p t j -> p (t j)"),
+                    banks[2 * bank_pair[0, 1] + q][:],
+                    ACT.Relu,
+                    bias=zero[:, 0:1],
+                )
+
+        def last_plane(pc, copy):
+            gather(3, *span(pc))
+            round_pair(copy, 2, *span(pc))
+
+        on_scalar, on_vector = nc.scalar.copy, nc.vector.tensor_copy
+        pieces = [(0, 0), (1, 0), (2, 0), (0, 1), (1, 1), (2, 1)]
+        for lo, hi in ((0, 256), (256, 768), (768, 1536)):
+            gather(0, lo, hi)
         for pc in pieces:
-            gather(1, pc)
-            round_pair(nc.scalar.copy, pc, 0)
+            gather(1, *span(pc))
+            round_pair(on_scalar, 0, *span(pc))
         for pc in pieces[:2]:
-            gather(2, pc)
+            gather(2, *span(pc))
         for s, pc in enumerate(pieces):
             if s >= 2:
-                gather(2, pc)
-            gather(3, pc)
-            round_pair(nc.scalar.copy if s < 4 else nc.vector.tensor_copy, pc, 2)
+                gather(2, *span(pc))
+            last_plane(pc, on_scalar if s < 4 else on_vector)
             if 2 <= s < 5:
                 relu_first_half(s - 2)
             project(pc)
             if 2 <= s < 5:
                 turn_and_add(s - 2)
-        for q in range(2):
-            nc.scalar.activation(
-                pooled[:, 2 * q : 2 * q + 2, :].rearrange("p t j -> p (t j)"),
-                banks[2 * bank_pair[0, 1] + q][:],
-                ACT.Relu,
-                bias=zero[:, 0:1],
-            )
+        relu_second_half()
         for nt in range(NT):
             finish(0, nt, banks[2 * sum_pair + nt // 2][:, HALF * (nt % 2) : HALF * (nt % 2 + 1)])
         for q in range(2):

@@ -22,6 +22,9 @@ PACK = 4
 STRIPE = 16
 HALF = 256
 NT = N // P
+GROUPS = 8
+CHUNK = 96
+CHUNKS = PICKS * J // CHUNK
 
 
 def tile_list_relus_silu_kernel(tc, xT, wgt, w_words, w_scales, b, offs, out):
@@ -32,7 +35,9 @@ def tile_list_relus_silu_kernel(tc, xT, wgt, w_words, w_scales, b, offs, out):
 
         offsets = keep.tile([P, PICKS * J // STRIPE], U16, name="offsets")
         planes = [keep.tile([P, T], F32, name=f"plane{i}") for i in range(PACK)]
-        strip = keep.tile([P, 26, HALF], F32, name="strip")
+        dealt = keep.tile([P, P], F32, name="dealt", align_bytes=64)
+        weights = keep.tile([P, PICKS * J], F32, name="weights", align_bytes=64)
+        strip = keep.tile([P, 14, HALF], F32, name="strip")
         w_codes = keep.tile([P, 2 * N], U8, name="w_codes", align_bytes=64)
         w_scale = keep.tile([P, N], U8, name="w_scale", align_bytes=64)
         bias = keep.tile([P, NT], F32, name="bias")
@@ -42,16 +47,15 @@ def tile_list_relus_silu_kernel(tc, xT, wgt, w_words, w_scales, b, offs, out):
         banks = [psum.tile([P, 2 * HALF], F32, name=f"bank{q}") for q in range(8)]
 
         nc.vector.memset(seed[:], 0.0)
+        nc.vector.memset(dealt[:, CHUNK:P], 0.0)
         nc.vector.memset(w_scale[:].bitcast(U32), 0)
         nc.scalar.activation(zero[:], seed[:], ACT.Silu)
         make_identity(nc, ident[:])
 
         x_planes = xT.rearrange("(p i) t -> i p t", i=PACK)
-        flat = strip[:].rearrange("p s j -> p (s j)")
+        nc.sync.dma_start(dealt[:, 0:CHUNK], wgt.rearrange("p (h j) -> (p h) j", h=2)[0 : 2 * P : STRIPE + 1, :])
         nc.sync.dma_start(planes[0][:], x_planes[0])
         nc.sync.dma_start(offsets[:], offs)
-        for lo, hi in ((0, 256), (256, 768), (768, 1536)):
-            nc.sync.dma_start(flat[:, lo:hi], wgt[:, lo:hi])
         for i in range(1, PACK):
             nc.sync.dma_start(planes[i][:], x_planes[i])
         nc.sync.dma_start(w_codes[:].bitcast(I32), w_words[0].bitcast(I32))
@@ -62,46 +66,84 @@ def tile_list_relus_silu_kernel(tc, xT, wgt, w_words, w_scales, b, offs, out):
         with nc.allow_non_contiguous_dma(reason="one bias value a partition"):
             nc.sync.dma_start(bias[:], b.rearrange("(t p) -> p t", p=P))
 
-        row = {0: range(14, 20), 1: range(20, 26), 2: (6, 2, 7, 4, 0, 1), 3: range(8, 14)}
-        bank_pair = {(0, 0): 0, (1, 0): 1, (2, 0): 3, (0, 1): 0, (1, 1): 1, (2, 1): 3}
-        sum_pair = 2
-        grouped = keep.tile([P, PICKS * J, PACK], BF16, name="grouped", align_bytes=64)
-        relus = [keep.tile([P, 2, N], F32, name=f"relus{c}") for c in range(PICKS)]
+        turned = banks[7][:, 0:P]
+        nc.tensor.transpose(turned, dealt[:], ident[:])
+
+        on_scalar, on_vector = nc.scalar.copy, nc.vector.tensor_copy
+        blocks = keep.tile([P, P], F32, name="blocks", align_bytes=64)
+        blocks_repeated = keep.tile([P, 14, 3, 2, STRIPE], F32, name="blocks_repeated", align_bytes=64)
+        nc.vector.transpose(blocks[:], dealt[:])
+        source = blocks[:, 0:CHUNK].rearrange("p (h g s) -> p s h g", h=3, g=2)
+        for lo, hi in ((0, 8), (10, 14)):
+            nc.vector.tensor_copy(
+                blocks_repeated[:, lo:hi], source[:, lo:hi, :, :].unsqueeze(4).to_broadcast([P, hi - lo, 3, 2, STRIPE])
+            )
+        for lo, hi in ((0, 256), (256, 768), (1024, 1280)):
+            nc.vector.transpose(weights[:, lo:hi], blocks_repeated[:].rearrange("p s h g r -> p (s h g r)")[:, lo:hi])
+
+        early = keep.tile([P, 4, 2, HALF], F32, name="early", align_bytes=64)
+        repeated = early[:].rearrange("p n k c -> p (n k) c")[:, :, 0:P]
+        for q, first in enumerate((8, 13)):
+            source = turned.rearrange("p (g s) -> p s g", g=GROUPS)[:, first : first + 3, :]
+            slots = repeated[:, 4 * q : 4 * q + 3, :]
+            on_scalar(slots.rearrange("p s (g r) -> p s g r", r=STRIPE), source.unsqueeze(3).to_broadcast([P, 3, GROUPS, STRIPE]))
+            for s in range(3):
+                nc.tensor.transpose(banks[q][:, CHUNK * s : CHUNK * s + P], slots[:, s, :], ident[:])
+            lo = 768 + J * q
+            on_scalar(weights[:, lo : lo + HALF], banks[q][:, lo - CHUNK * first : lo - CHUNK * first + HALF])
+
+        flat = strip[:].rearrange("p s j -> p (s j)")
+        relus = [keep.tile([P, 2, N], F32, name=f"relus{c}", align_bytes=64) for c in range(PICKS)]
         pooled = keep.tile([P, NT, HALF], F32, name="pooled")
         result = [keep.tile([P, NT, HALF], F32, name=f"result{h}") for h in range(2)]
         out_rows = out.rearrange("(t p) j -> p t j", p=P)
+        A0, B0, A1, B1, A2, B2 = range(6)
+        grouped = {pc: early[:, n].rearrange("p k c -> p (k c)").bitcast(BF16).rearrange("p (j i) -> p j i", i=PACK) for n, pc in enumerate((A0, A1, A2, B0))}
+        grouped[B2] = keep.tile([P, HALF, PACK], BF16, name="grouped_last", align_bytes=64)[:]
+        fifth = keep.tile([P, 2 * HALF], F32, name="fifth", align_bytes=64)
+        nc.vector.memset(fifth[:, 0:8], 0.0)
+        grouped[B1] = fifth[:].bitcast(BF16).rearrange("p (j i) -> p j i", i=PACK)
+        codes = [keep.tile([P, HALF], U32, name=f"codes{pc}", align_bytes=64) for pc in range(6)]
+        scales = [keep.tile([P, HALF], U8, name=f"scales{pc}", align_bytes=64) for pc in range(6)]
+        rows = {A0: (0, 4, 8, 9), B0: (1, 5, 8, 9), A1: (2, 6, 10, 11), A2: (3, 7, 12, 13), B1: (10, 11, 12, 13), B2: (8, 9, 10, 11)}
+        pair_of = {A0: 0, A1: 1, A2: 3, B0: 0, B1: 1, B2: 3}
+        sum_pair = 2
 
         def gather(i, lo, hi):
-            first = row[i][lo // HALF] * HALF
+            first = rows[lo // HALF][i] * HALF + lo % HALF
             nc.vector.tensor_tensor(
                 flat[:, first : first + hi - lo],
                 planes[i][:].indirect(offsets[:, lo // STRIPE : hi // STRIPE]),
-                flat[:, lo:hi],
+                weights[:, lo:hi],
                 ALU.mult,
             )
 
-        def round_pair(copy, i, lo, hi):
-            r0, r1 = row[i][lo // HALF], row[i + 1][lo // HALF]
-            both = strip[:, r0 : r1 + 1 : r1 - r0, :]
-            copy(grouped[:, lo:hi, i : i + 2], both.rearrange("p i j -> p j i"))
+        def gather_piece(i, pc):
+            gather(i, pc * HALF, (pc + 1) * HALF)
 
-        def span(pc):
-            return pc[0] * J + pc[1] * HALF, pc[0] * J + (pc[1] + 1) * HALF
+        def round_pair(i, pc):
+            r0, r1 = rows[pc][i], rows[pc][i + 1]
+            on_scalar(grouped[pc][:, :, i : i + 2], strip[:, r0 : r1 + 1 : r1 - r0, :].rearrange("p i j -> p j i"))
+
+        def round_four(copy, pc, lo, hi):
+            r0 = rows[pc][0]
+            copy(grouped[pc][:, lo:hi, :], strip[:, r0 : r0 + PACK, lo:hi].rearrange("p i j -> p j i"))
+
+        def quantise(pc, lo=0, hi=HALF):
+            nc.vector.quantize_mx(
+                out=codes[pc][:, lo:hi].bitcast(FP8X4),
+                scales=scales[pc][:, lo:hi],
+                in_=grouped[pc][:, lo:hi, :].rearrange("p j i -> p (j i)"),
+            )
 
         def project(pc):
-            name = f"{pc[0]}{pc[1]}"
-            codes = keep.tile([P, HALF], U32, name="codes" + name, align_bytes=64)
-            scales = keep.tile([P, HALF], U8, name="scales" + name, align_bytes=64)
-            nc.vector.quantize_mx(
-                out=codes[:].bitcast(FP8X4), scales=scales[:], in_=grouped[:, span(pc)[0] : span(pc)[1], :].rearrange("p j i -> p (j i)")
-            )
-            pair = banks[2 * bank_pair[pc] : 2 * bank_pair[pc] + 2]
-            if pc[1] == 0:
+            pair = banks[2 * pair_of[pc] : 2 * pair_of[pc] + 2]
+            if pc % 2 == 0:
                 for jt in range(2):
                     nc.tensor.matmul_mx(
                         out=pair[jt][:],
-                        lhsT=codes[:, P * jt : P * (jt + 1)].bitcast(FP8X4),
-                        lhsT_scale=scales[:, P * jt : P * (jt + 1)],
+                        lhsT=codes[pc][:, P * jt : P * (jt + 1)].bitcast(FP8X4),
+                        lhsT_scale=scales[pc][:, P * jt : P * (jt + 1)],
                         rhs=w_codes[:].bitcast(FP4X4),
                         rhs_scale=w_scale[:],
                         start=True,
@@ -113,28 +155,25 @@ def tile_list_relus_silu_kernel(tc, xT, wgt, w_words, w_scales, b, offs, out):
                         out=pair[nt // 2][:, HALF * (nt % 2) : HALF * (nt % 2 + 1)],
                         lhsT=w_codes[:, 2 * P * nt : 2 * P * (nt + 1)].bitcast(FP4X4),
                         lhsT_scale=w_scale[:, P * nt : P * (nt + 1)],
-                        rhs=codes[:].bitcast(FP8X4),
-                        rhs_scale=scales[:],
+                        rhs=codes[pc][:].bitcast(FP8X4),
+                        rhs_scale=scales[pc][:],
                         start=True,
                         stop=True,
                     )
 
-        def relu_first_half(c):
-            for jt in range(2):
-                nc.scalar.activation(relus[c][:, jt, :], banks[2 * bank_pair[c, 0] + jt][:], ACT.Relu, bias=zero[:, 0:1])
-
-        def turn_and_add(c):
-            for jt in range(2):
-                for nt in range(NT):
-                    col = HALF * (nt % 2) + P * jt
-                    nc.tensor.matmul(
-                        banks[2 * sum_pair + nt // 2][:, col : col + P],
-                        relus[c][:, jt, P * nt : P * (nt + 1)],
-                        ident[:],
-                        start=(c == 0 and col == 0),
-                        stop=(c == PICKS - 1 and col == 2 * HALF - P),
-                        is_transpose=True,
-                    )
+        def relu_and_add(pc, jt):
+            c = pc // 2
+            nc.scalar.activation(relus[c][:, jt, :], banks[2 * pair_of[pc] + jt][:], ACT.Relu, bias=(fifth if (pc, jt) == (A1, 0) else zero)[:, 0:1])
+            for nt in range(NT):
+                col = HALF * (nt % 2) + P * jt
+                nc.tensor.matmul(
+                    banks[2 * sum_pair + nt // 2][:, col : col + P],
+                    relus[c][:, jt, P * nt : P * (nt + 1)],
+                    ident[:],
+                    start=(c == 0 and col == 0),
+                    stop=(c == PICKS - 1 and col == 2 * HALF - P),
+                    is_transpose=True,
+                )
 
         def finish(h, nt, source):
             nc.scalar.activation(result[h][:, nt, :], source, ACT.Silu, bias=bias[:, nt : nt + 1])
@@ -146,45 +185,62 @@ def tile_list_relus_silu_kernel(tc, xT, wgt, w_words, w_scales, b, offs, out):
             elif nt % 2 == 1:
                 nc.sync.dma_start(out_rows[:, nt - 1 : nt + 1, cols], result[h][:, nt - 1 : nt + 1, :])
 
-        def relu_second_half():
-            for q in range(2):
-                nc.scalar.activation(
-                    pooled[:, 2 * q : 2 * q + 2, :].rearrange("p t j -> p (t j)"),
-                    banks[2 * bank_pair[0, 1] + q][:],
-                    ACT.Relu,
-                    bias=zero[:, 0:1],
-                )
+        def pooled_pair(q):
+            return pooled[:, 2 * q : 2 * q + 2, :].rearrange("p t j -> p (t j)")
 
-        def last_plane(pc, copy):
-            gather(3, *span(pc))
-            round_pair(copy, 2, *span(pc))
-
-        on_scalar, on_vector = nc.scalar.copy, nc.vector.tensor_copy
-        pieces = [(0, 0), (1, 0), (2, 0), (0, 1), (1, 1), (2, 1)]
-        for lo, hi in ((0, 256), (256, 768), (768, 1536)):
+        for lo, hi in ((0, 256), (256, 768), (1024, 1280)):
             gather(0, lo, hi)
-        for pc in pieces:
-            gather(1, *span(pc))
-            round_pair(on_scalar, 0, *span(pc))
-        for pc in pieces[:2]:
-            gather(2, *span(pc))
-        for s, pc in enumerate(pieces):
-            if s >= 2:
-                gather(2, *span(pc))
-            last_plane(pc, on_scalar if s < 4 else on_vector)
-            if 2 <= s < 5:
-                relu_first_half(s - 2)
-            project(pc)
-            if 2 <= s < 5:
-                turn_and_add(s - 2)
-        relu_second_half()
+        for lo, hi in ((0, 256), (256, 768), (1024, 1280)):
+            gather(1, lo, hi)
+        for pc in (A0, A1, A2, B0):
+            round_pair(0, pc)
+        for i in (2, 3):
+            for pc in (A0, A1, A2):
+                gather_piece(i, pc)
+        for pc in (A0, A1, A2):
+            round_pair(2, pc)
+        quantise(A0)
+        project(A0)
+        gather_piece(2, B0)
+        gather_piece(3, B0)
+        quantise(A1)
+        project(A1)
+        gather_piece(0, B1)
+        gather_piece(1, B1)
+        quantise(A2)
+        project(A2)
+        gather_piece(2, B1)
+        gather_piece(3, B1)
+        relu_and_add(A0, 0)
+        relu_and_add(A0, 1)
+        round_pair(2, B0)
+        quantise(B0)
+        project(B0)
+        gather_piece(0, B2)
+        gather_piece(1, B2)
+        relu_and_add(A1, 0)
+        relu_and_add(A1, 1)
+        round_four(on_scalar, B1, 0, HALF)
+        quantise(B1)
+        project(B1)
+        relu_and_add(A2, 0)
+        relu_and_add(A2, 1)
+        for lo in (0, P):
+            for i in (2, 3):
+                gather(i, B2 * HALF + lo, B2 * HALF + lo + P)
+        for lo in (0, P):
+            round_four(on_vector, B2, lo, lo + P)
+        for lo in (0, P):
+            quantise(B2, lo, lo + P)
+        project(B2)
+        for q in range(2):
+            nc.scalar.activation(pooled_pair(q), banks[2 * pair_of[B0] + q][:], ACT.Relu, bias=zero[:, 0:1])
         for nt in range(NT):
             finish(0, nt, banks[2 * sum_pair + nt // 2][:, HALF * (nt % 2) : HALF * (nt % 2 + 1)])
         for q in range(2):
-            part = pooled[:, 2 * q : 2 * q + 2, :].rearrange("p t j -> p (t j)")
-            nc.vector.scalar_tensor_tensor(part, banks[2 * bank_pair[1, 1] + q][:], 0.0, part, ALU.max, ALU.add)
+            nc.vector.scalar_tensor_tensor(pooled_pair(q), banks[2 * pair_of[B1] + q][:], 0.0, pooled_pair(q), ALU.max, ALU.add)
         for nt in range(NT):
             part = pooled[:, nt, :]
-            source = banks[2 * bank_pair[2, 1] + nt // 2][:, HALF * (nt % 2) : HALF * (nt % 2 + 1)]
+            source = banks[2 * pair_of[B2] + nt // 2][:, HALF * (nt % 2) : HALF * (nt % 2 + 1)]
             nc.vector.scalar_tensor_tensor(part, source, 0.0, part, ALU.max, ALU.add)
             finish(1, nt, part)

@@ -103,6 +103,8 @@ def tile_list_relus_silu_kernel(tc, xT, wgt, w_words, w_scales, b, offs, out):
         fifth = keep.tile([P, 2 * HALF], F32, name="fifth", align_bytes=64)
         nc.vector.memset(fifth[:, 0:8], 0.0)
         grouped[B1] = fifth[:].bitcast(BF16).rearrange("p (j i) -> p j i", i=PACK)
+        nc.vector.memset(early[:, 3, 1, 1:2], 0.0)
+        zero_for = {(A0, 0): early[:, 3, 1, 1:2], (A1, 0): fifth[:, 0:1]}
         codes = [keep.tile([P, HALF], U32, name=f"codes{pc}", align_bytes=64) for pc in range(6)]
         scales = [keep.tile([P, HALF], U8, name=f"scales{pc}", align_bytes=64) for pc in range(6)]
         rows = {A0: (0, 4, 8, 9), B0: (1, 5, 8, 9), A1: (2, 6, 10, 11), A2: (3, 7, 12, 13), B1: (10, 11, 12, 13), B2: (8, 9, 10, 11)}
@@ -121,13 +123,16 @@ def tile_list_relus_silu_kernel(tc, xT, wgt, w_words, w_scales, b, offs, out):
         def gather_piece(i, pc):
             gather(i, pc * HALF, (pc + 1) * HALF)
 
-        def round_pair(i, pc):
+        def round_pair(i, pc, lo=0, hi=HALF):
             r0, r1 = rows[pc][i], rows[pc][i + 1]
-            on_scalar(grouped[pc][:, :, i : i + 2], strip[:, r0 : r1 + 1 : r1 - r0, :].rearrange("p i j -> p j i"))
+            on_scalar(grouped[pc][:, lo:hi, i : i + 2], strip[:, r0 : r1 + 1 : r1 - r0, lo:hi].rearrange("p i j -> p j i"))
 
         def round_four(copy, pc, lo, hi):
             r0 = rows[pc][0]
-            copy(grouped[pc][:, lo:hi, :], strip[:, r0 : r0 + PACK, lo:hi].rearrange("p i j -> p j i"))
+            copy(
+                grouped[pc][:, lo:hi, :].rearrange("p (c j) i -> p c i j", j=4),
+                strip[:, r0 : r0 + PACK, lo:hi].rearrange("p i (c j) -> p c i j", j=4),
+            )
 
         def quantise(pc, lo=0, hi=HALF):
             nc.vector.quantize_mx(
@@ -163,7 +168,7 @@ def tile_list_relus_silu_kernel(tc, xT, wgt, w_words, w_scales, b, offs, out):
 
         def relu_and_add(pc, jt):
             c = pc // 2
-            nc.scalar.activation(relus[c][:, jt, :], banks[2 * pair_of[pc] + jt][:], ACT.Relu, bias=(fifth if (pc, jt) == (A1, 0) else zero)[:, 0:1])
+            nc.scalar.activation(relus[c][:, jt, :], banks[2 * pair_of[pc] + jt][:], ACT.Relu, bias=zero_for.get((pc, jt), zero[:, 0:1]))
             for nt in range(NT):
                 col = HALF * (nt % 2) + P * jt
                 nc.tensor.matmul(
@@ -194,12 +199,17 @@ def tile_list_relus_silu_kernel(tc, xT, wgt, w_words, w_scales, b, offs, out):
             gather(1, lo, hi)
         for pc in (A0, A1, A2, B0):
             round_pair(0, pc)
-        for i in (2, 3):
-            for pc in (A0, A1, A2):
-                gather_piece(i, pc)
         for pc in (A0, A1, A2):
+            gather_piece(2, pc)
+        for lo in (0, P):
+            gather(3, lo, lo + P)
+            round_pair(2, A0, lo, lo + P)
+        gather_piece(3, A1)
+        quantise(A0, 0, P)
+        gather_piece(3, A2)
+        quantise(A0, P, HALF)
+        for pc in (A1, A2):
             round_pair(2, pc)
-        quantise(A0)
         project(A0)
         gather_piece(2, B0)
         gather_piece(3, B0)

@@ -54,9 +54,8 @@ def tile_list_relus_silu_kernel(tc, xT, wgt, w_words, w_scales, b, offs, out):
 
         x_planes = xT.rearrange("(p i) t -> i p t", i=PACK)
         nc.sync.dma_start(dealt[:, 0:CHUNK], wgt.rearrange("p (h j) -> (p h) j", h=2)[0 : 2 * P : STRIPE + 1, :])
-        nc.sync.dma_start(planes[0][:], x_planes[0])
         nc.sync.dma_start(offsets[:], offs)
-        for i in range(1, PACK):
+        for i in range(PACK):
             nc.sync.dma_start(planes[i][:], x_planes[i])
         nc.sync.dma_start(w_codes[:].bitcast(I32), w_words[0].bitcast(I32))
         for q in range(4):
@@ -141,6 +140,11 @@ def tile_list_relus_silu_kernel(tc, xT, wgt, w_words, w_scales, b, offs, out):
                 in_=grouped[pc][:, lo:hi, :].rearrange("p j i -> p (j i)"),
             )
 
+        def product(pc, nt):
+            if pc == B2:
+                return banks[(0, 1, 6, 7)[nt]][:, 0:HALF]
+            return banks[2 * pair_of[pc] + nt // 2][:, HALF * (nt % 2) : HALF * (nt % 2 + 1)]
+
         def project(pc):
             pair = banks[2 * pair_of[pc] : 2 * pair_of[pc] + 2]
             if pc % 2 == 0:
@@ -157,7 +161,7 @@ def tile_list_relus_silu_kernel(tc, xT, wgt, w_words, w_scales, b, offs, out):
             else:
                 for nt in range(NT):
                     nc.tensor.matmul_mx(
-                        out=pair[nt // 2][:, HALF * (nt % 2) : HALF * (nt % 2 + 1)],
+                        out=product(pc, nt),
                         lhsT=w_codes[:, 2 * P * nt : 2 * P * (nt + 1)].bitcast(FP4X4),
                         lhsT_scale=w_scale[:, P * nt : P * (nt + 1)],
                         rhs=codes[pc][:].bitcast(FP8X4),
@@ -242,15 +246,15 @@ def tile_list_relus_silu_kernel(tc, xT, wgt, w_words, w_scales, b, offs, out):
             round_four(on_vector, B2, lo, lo + P)
         for lo in (0, P):
             quantise(B2, lo, lo + P)
-        project(B2)
         for q in range(2):
             nc.scalar.activation(pooled_pair(q), banks[2 * pair_of[B0] + q][:], ACT.Relu, bias=zero[:, 0:1])
+        project(B2)
         for nt in range(NT):
             finish(0, nt, banks[2 * sum_pair + nt // 2][:, HALF * (nt % 2) : HALF * (nt % 2 + 1)])
         for q in range(2):
             nc.vector.scalar_tensor_tensor(pooled_pair(q), banks[2 * pair_of[B1] + q][:], 0.0, pooled_pair(q), ALU.max, ALU.add)
         for nt in range(NT):
             part = pooled[:, nt, :]
-            source = banks[2 * pair_of[B2] + nt // 2][:, HALF * (nt % 2) : HALF * (nt % 2 + 1)]
+            source = product(B2, nt)
             nc.vector.scalar_tensor_tensor(part, source, 0.0, part, ALU.max, ALU.add)
             finish(1, nt, part)

@@ -77,7 +77,7 @@ def tile_list_relus_silu_kernel(tc, xT, wgt, w_words, w_scales, b, offs, out):
             nc.vector.tensor_copy(
                 blocks_repeated[:, lo:hi], source[:, lo:hi, :, :].unsqueeze(4).to_broadcast([P, hi - lo, 3, 2, STRIPE])
             )
-        for lo, hi in ((0, 256), (256, 768), (1024, 1280)):
+        for lo, hi in ((0, 768), (1024, 1280)):
             nc.vector.transpose(weights[:, lo:hi], blocks_repeated[:].rearrange("p s h g r -> p (s h g r)")[:, lo:hi])
 
         early = keep.tile([P, 4, 2, HALF], F32, name="early", align_bytes=64)
@@ -197,7 +197,7 @@ def tile_list_relus_silu_kernel(tc, xT, wgt, w_words, w_scales, b, offs, out):
         def pooled_pair(q):
             return pooled[:, 2 * q : 2 * q + 2, :].rearrange("p t j -> p (t j)")
 
-        for lo, hi in ((0, 256), (256, 768), (1024, 1280)):
+        for lo, hi in ((0, 768), (1024, 1280)):
             gather(0, lo, hi)
         for lo, hi in ((0, 256), (256, 768), (1024, 1280)):
             gather(1, lo, hi)

@@ -98,16 +98,16 @@ def tile_list_relus_silu_kernel(tc, xT, wgt, w_words, w_scales, b, offs, out):
         out_rows = out.rearrange("(t p) j -> p t j", p=P)
         A0, B0, A1, B1, A2, B2 = range(6)
         grouped = {pc: early[:, n].rearrange("p k c -> p (k c)").bitcast(BF16).rearrange("p (j i) -> p j i", i=PACK) for n, pc in enumerate((A0, A1, A2, B0))}
-        grouped[B2] = keep.tile([P, HALF, PACK], BF16, name="grouped_last", align_bytes=64)[:]
         fifth = keep.tile([P, 2 * HALF], F32, name="fifth", align_bytes=64)
-        nc.vector.memset(fifth[:, 0:8], 0.0)
+        nc.vector.memset(fifth[:, HALF - 8 : HALF + 8], 0.0)
         grouped[B1] = fifth[:].bitcast(BF16).rearrange("p (j i) -> p j i", i=PACK)
+        grouped[B2] = grouped[B1]
         nc.vector.memset(early[:, 3, 1, 1:2], 0.0)
-        zero_for = {(A0, 0): early[:, 3, 1, 1:2], (A1, 0): fifth[:, 0:1]}
+        zero_for = {(A0, 0): early[:, 3, 1, 1:2], (A1, 0): fifth[:, HALF - 1 : HALF], (A1, 1): fifth[:, HALF : HALF + 1]}
         codes = [keep.tile([P, HALF], U32, name=f"codes{pc}", align_bytes=64) for pc in range(6)]
         scales = [keep.tile([P, HALF], U8, name=f"scales{pc}", align_bytes=64) for pc in range(6)]
         rows = {A0: (0, 4, 8, 9), B0: (1, 5, 8, 9), A1: (2, 6, 10, 11), A2: (3, 7, 12, 13), B1: (10, 11, 12, 13), B2: (8, 9, 10, 11)}
-        pair_of = {A0: 0, A1: 1, A2: 3, B0: 0, B1: 1, B2: 3}
+        pair_of = {A0: 0, A1: 1, A2: 3, B0: 0, B1: 3, B2: 0}
         sum_pair = 2
 
         def gather(i, lo, hi):
@@ -142,10 +142,10 @@ def tile_list_relus_silu_kernel(tc, xT, wgt, w_words, w_scales, b, offs, out):
 
         def product(pc, nt):
             if pc == B2:
-                return banks[(0, 1, 6, 7)[nt]][:, 0:HALF]
+                return banks[nt][:, 0:HALF]
             return banks[2 * pair_of[pc] + nt // 2][:, HALF * (nt % 2) : HALF * (nt % 2 + 1)]
 
-        def project(pc):
+        def project(pc, blocks=range(NT)):
             pair = banks[2 * pair_of[pc] : 2 * pair_of[pc] + 2]
             if pc % 2 == 0:
                 for jt in range(2):
@@ -159,7 +159,7 @@ def tile_list_relus_silu_kernel(tc, xT, wgt, w_words, w_scales, b, offs, out):
                         stop=True,
                     )
             else:
-                for nt in range(NT):
+                for nt in blocks:
                     nc.tensor.matmul_mx(
                         out=product(pc, nt),
                         lhsT=w_codes[:, 2 * P * nt : 2 * P * (nt + 1)].bitcast(FP4X4),
@@ -234,11 +234,12 @@ def tile_list_relus_silu_kernel(tc, xT, wgt, w_words, w_scales, b, offs, out):
         gather_piece(1, B2)
         relu_and_add(A1, 0)
         relu_and_add(A1, 1)
-        round_four(on_scalar, B1, 0, HALF)
+        for lo in (0, P):
+            round_four(on_scalar, B1, lo, lo + P)
         quantise(B1)
-        project(B1)
-        relu_and_add(A2, 0)
-        relu_and_add(A2, 1)
+        for jt in range(2):
+            relu_and_add(A2, jt)
+            project(B1, (2 * jt, 2 * jt + 1))
         for lo in (0, P):
             for i in (2, 3):
                 gather(i, B2 * HALF + lo, B2 * HALF + lo + P)

@@ -73,11 +73,9 @@ def tile_list_relus_silu_kernel(tc, xT, wgt, w_words, w_scales, b, offs, out):
         blocks_repeated = keep.tile([P, 14, 3, 2, STRIPE], F32, name="blocks_repeated", align_bytes=64)
         nc.vector.transpose(blocks[:], dealt[:])
         source = blocks[:, 0:CHUNK].rearrange("p (h g s) -> p s h g", h=3, g=2)
-        for lo, hi in ((0, 8), (10, 14)):
-            nc.vector.tensor_copy(
-                blocks_repeated[:, lo:hi], source[:, lo:hi, :, :].unsqueeze(4).to_broadcast([P, hi - lo, 3, 2, STRIPE])
-            )
-        for lo, hi in ((0, 768), (1024, 1280)):
+        for copy, lo, hi in ((on_vector, 0, 3), (on_scalar, 3, 8), (on_scalar, 10, 14)):
+            copy(blocks_repeated[:, lo:hi], source[:, lo:hi, :, :].unsqueeze(4).to_broadcast([P, hi - lo, 3, 2, STRIPE]))
+        for lo, hi in ((0, 256), (256, 768), (1024, 1280)):
             nc.vector.transpose(weights[:, lo:hi], blocks_repeated[:].rearrange("p s h g r -> p (s h g r)")[:, lo:hi])
 
         early = keep.tile([P, 4, 2, HALF], F32, name="early", align_bytes=64)

@@ -37,7 +37,7 @@ def tile_list_relus_silu_kernel(tc, xT, wgt, w_words, w_scales, b, offs, out):
         planes = [keep.tile([P, T], F32, name=f"plane{i}") for i in range(PACK)]
         dealt = keep.tile([P, P], F32, name="dealt", align_bytes=64)
         weights = keep.tile([P, PICKS * J], F32, name="weights", align_bytes=64)
-        strip = keep.tile([P, 14, HALF], F32, name="strip")
+        flat = keep.tile([P, 15 * HALF], F32, name="flat")
         w_codes = keep.tile([P, 2 * N], U8, name="w_codes", align_bytes=64)
         w_scale = keep.tile([P, N], U8, name="w_scale", align_bytes=64)
         bias = keep.tile([P, NT], F32, name="bias")
@@ -89,7 +89,7 @@ def tile_list_relus_silu_kernel(tc, xT, wgt, w_words, w_scales, b, offs, out):
             lo = 768 + J * q
             on_scalar(weights[:, lo : lo + HALF], banks[q][:, lo - CHUNK * first : lo - CHUNK * first + HALF])
 
-        flat = strip[:].rearrange("p s j -> p (s j)")
+        late_rows = flat[:, HALF : 15 * HALF].rearrange("p (s j) -> p s j", j=HALF)
         relus = [keep.tile([P, 2, N], F32, name=f"relus{c}", align_bytes=64) for c in range(PICKS)]
         pooled = keep.tile([P, NT, HALF], F32, name="pooled")
         result = [keep.tile([P, NT, HALF], F32, name=f"result{h}") for h in range(2)]
@@ -105,11 +105,14 @@ def tile_list_relus_silu_kernel(tc, xT, wgt, w_words, w_scales, b, offs, out):
         codes = [keep.tile([P, HALF], U32, name=f"codes{pc}", align_bytes=64) for pc in range(6)]
         scales = [keep.tile([P, HALF], U8, name=f"scales{pc}", align_bytes=64) for pc in range(6)]
         rows = {A0: (0, 4, 8, 9), B0: (1, 5, 8, 9), A1: (2, 6, 10, 11), A2: (3, 7, 12, 13), B1: (10, 11, 12, 13), B2: (8, 9, 10, 11)}
+        column = {(pc, i): HALF * r + (HALF if r >= 8 else 0) for pc in rows for i, r in enumerate(rows[pc])}
+        column[A0, 2] -= HALF
+        column[A0, 3] -= P
         pair_of = {A0: 0, A1: 1, A2: 3, B0: 0, B1: 3, B2: 0}
         sum_pair = 2
 
         def gather(i, lo, hi):
-            first = rows[lo // HALF][i] * HALF + lo % HALF
+            first = column[lo // HALF, i] + lo % HALF
             nc.vector.tensor_tensor(
                 flat[:, first : first + hi - lo],
                 planes[i][:].indirect(offsets[:, lo // STRIPE : hi // STRIPE]),
@@ -121,14 +124,15 @@ def tile_list_relus_silu_kernel(tc, xT, wgt, w_words, w_scales, b, offs, out):
             gather(i, pc * HALF, (pc + 1) * HALF)
 
         def round_pair(i, pc, lo=0, hi=HALF):
-            r0, r1 = rows[pc][i], rows[pc][i + 1]
-            on_scalar(grouped[pc][:, lo:hi, i : i + 2], strip[:, r0 : r1 + 1 : r1 - r0, lo:hi].rearrange("p i j -> p j i"))
+            c0, c1 = column[pc, i], column[pc, i + 1]
+            both = flat[:, c0 : c0 + 2 * (c1 - c0)].rearrange("p (i j) -> p j i", i=2)
+            on_scalar(grouped[pc][:, lo:hi, i : i + 2], both[:, lo:hi, :])
 
         def round_four(copy, pc, lo, hi):
             r0 = rows[pc][0]
             copy(
                 grouped[pc][:, lo:hi, :].rearrange("p (c j) i -> p c i j", j=4),
-                strip[:, r0 : r0 + PACK, lo:hi].rearrange("p i (c j) -> p c i j", j=4),
+                late_rows[:, r0 : r0 + PACK, lo:hi].rearrange("p i (c j) -> p c i j", j=4),
             )
 
         def quantise(pc, lo=0, hi=HALF):
@@ -201,7 +205,8 @@ def tile_list_relus_silu_kernel(tc, xT, wgt, w_words, w_scales, b, offs, out):
             gather(1, lo, hi)
         for pc in (A0, A1, A2, B0):
             round_pair(0, pc)
-        for pc in (A0, A1, A2):
+        gather(2, 0, HALF + P)
+        for pc in (A1, A2):
             gather_piece(2, pc)
         for lo in (0, P):
             gather(3, lo, lo + P)
@@ -213,7 +218,7 @@ def tile_list_relus_silu_kernel(tc, xT, wgt, w_words, w_scales, b, offs, out):
         for pc in (A1, A2):
             round_pair(2, pc)
         project(A0)
-        gather_piece(2, B0)
+        gather(2, HALF + P, 2 * HALF)
         gather_piece(3, B0)
         quantise(A1)
         project(A1)

@@ -89,26 +89,25 @@ def tile_list_relus_silu_kernel(tc, xT, wgt, w_words, w_scales, b, offs, out):
             lo = 768 + J * q
             on_scalar(weights[:, lo : lo + HALF], banks[q][:, lo - CHUNK * first : lo - CHUNK * first + HALF])
 
-        late_rows = flat[:, HALF : 15 * HALF].rearrange("p (s j) -> p s j", j=HALF)
+        late_rows = flat[:].rearrange("p (s j) -> p s j", j=HALF)
         relus = [keep.tile([P, 2, N], F32, name=f"relus{c}", align_bytes=64) for c in range(PICKS)]
         pooled = keep.tile([P, NT, HALF], F32, name="pooled")
         result = [keep.tile([P, NT, HALF], F32, name=f"result{h}") for h in range(2)]
         out_rows = out.rearrange("(t p) j -> p t j", p=P)
         A0, B0, A1, B1, A2, B2 = range(6)
-        grouped = {pc: early[:, n].rearrange("p k c -> p (k c)").bitcast(BF16).rearrange("p (j i) -> p j i", i=PACK) for n, pc in enumerate((A0, A1, A2, B0))}
+        grouped = {pc: early[:, n].rearrange("p k c -> p (k c)").bitcast(BF16).rearrange("p (j i) -> p j i", i=PACK) for n, pc in enumerate((A0, A1, B0, A2))}
         fifth = keep.tile([P, 2 * HALF], F32, name="fifth", align_bytes=64)
         nc.vector.memset(fifth[:, HALF - 8 : HALF + 8], 0.0)
         grouped[B1] = fifth[:].bitcast(BF16).rearrange("p (j i) -> p j i", i=PACK)
         grouped[B2] = grouped[B1]
         nc.vector.memset(early[:, 3, 1, 1:2], 0.0)
-        zero_for = {(A0, 0): early[:, 3, 1, 1:2], (A1, 0): fifth[:, HALF - 1 : HALF], (A1, 1): fifth[:, HALF : HALF + 1]}
+        zero_for = {(A0, 0): early[:, 3, 1, 1:2], (A1, 1): fifth[:, HALF - 1 : HALF], (B0, 1): fifth[:, HALF : HALF + 1]}
         codes = [keep.tile([P, HALF], U32, name=f"codes{pc}", align_bytes=64) for pc in range(6)]
         scales = [keep.tile([P, HALF], U8, name=f"scales{pc}", align_bytes=64) for pc in range(6)]
-        rows = {A0: (0, 4, 8, 9), B0: (1, 5, 8, 9), A1: (2, 6, 10, 11), A2: (3, 7, 12, 13), B1: (10, 11, 12, 13), B2: (8, 9, 10, 11)}
-        column = {(pc, i): HALF * r + (HALF if r >= 8 else 0) for pc in rows for i, r in enumerate(rows[pc])}
-        column[A0, 2] -= HALF
-        column[A0, 3] -= P
-        pair_of = {A0: 0, A1: 1, A2: 3, B0: 0, B1: 3, B2: 0}
+        rows = {A0: (0, 4, 9, 8), B0: (1, 5, 10, 12), A1: (2, 6, 11, 13), A2: (3, 7, 8, 9), B1: (10, 11, 12, 13), B2: (8, 9, 10, 11)}
+        column = {(pc, i): HALF * r for pc in rows for i, r in enumerate(rows[pc])}
+        pair_of = {A0: 0, A1: 1, A2: 0, B0: 3, B1: 0}
+        last_banks = (2, 3, 6, 7)
         sum_pair = 2
 
         def gather(i, lo, hi):
@@ -124,9 +123,9 @@ def tile_list_relus_silu_kernel(tc, xT, wgt, w_words, w_scales, b, offs, out):
             gather(i, pc * HALF, (pc + 1) * HALF)
 
         def round_pair(i, pc, lo=0, hi=HALF):
-            c0, c1 = column[pc, i], column[pc, i + 1]
+            c0, c1 = sorted((column[pc, i], column[pc, i + 1]))
             both = flat[:, c0 : c0 + 2 * (c1 - c0)].rearrange("p (i j) -> p j i", i=2)
-            on_scalar(grouped[pc][:, lo:hi, i : i + 2], both[:, lo:hi, :])
+            on_scalar(grouped[pc][:, lo:hi, i : i + 2], both[:, lo:hi, :: 1 if c0 == column[pc, i] else -1])
 
         def round_four(copy, pc, lo, hi):
             r0 = rows[pc][0]
@@ -144,12 +143,12 @@ def tile_list_relus_silu_kernel(tc, xT, wgt, w_words, w_scales, b, offs, out):
 
         def product(pc, nt):
             if pc == B2:
-                return banks[nt][:, 0:HALF]
+                return banks[last_banks[nt]][:, 0:HALF]
             return banks[2 * pair_of[pc] + nt // 2][:, HALF * (nt % 2) : HALF * (nt % 2 + 1)]
 
         def project(pc, blocks=range(NT)):
-            pair = banks[2 * pair_of[pc] : 2 * pair_of[pc] + 2]
             if pc % 2 == 0:
+                pair = banks[2 * pair_of[pc] : 2 * pair_of[pc] + 2]
                 for jt in range(2):
                     nc.tensor.matmul_mx(
                         out=pair[jt][:],
@@ -199,59 +198,60 @@ def tile_list_relus_silu_kernel(tc, xT, wgt, w_words, w_scales, b, offs, out):
         def pooled_pair(q):
             return pooled[:, 2 * q : 2 * q + 2, :].rearrange("p t j -> p (t j)")
 
+        def first_relu(q):
+            nc.scalar.activation(pooled_pair(q), banks[2 * pair_of[B0] + q][:], ACT.Relu, bias=zero_for.get((B0, q), zero[:, 0:1]))
+
         for lo, hi in ((0, 768), (1024, 1280)):
             gather(0, lo, hi)
         for lo, hi in ((0, 256), (256, 768), (1024, 1280)):
             gather(1, lo, hi)
         for pc in (A0, A1, A2, B0):
             round_pair(0, pc)
-        gather(2, 0, HALF + P)
-        for pc in (A1, A2):
-            gather_piece(2, pc)
+        gather(2, 0, 3 * HALF)
         for lo in (0, P):
             gather(3, lo, lo + P)
             round_pair(2, A0, lo, lo + P)
         gather_piece(3, A1)
         quantise(A0, 0, P)
-        gather_piece(3, A2)
+        gather_piece(3, B0)
         quantise(A0, P, HALF)
-        for pc in (A1, A2):
+        for pc in (A1, B0):
             round_pair(2, pc)
         project(A0)
-        gather(2, HALF + P, 2 * HALF)
-        gather_piece(3, B0)
+        gather_piece(2, A2)
+        gather_piece(3, A2)
         quantise(A1)
         project(A1)
-        gather_piece(0, B1)
         gather_piece(1, B1)
-        quantise(A2)
-        project(A2)
-        gather_piece(2, B1)
         gather_piece(3, B1)
-        relu_and_add(A0, 0)
-        relu_and_add(A0, 1)
-        round_pair(2, B0)
         quantise(B0)
         project(B0)
+        gather_piece(0, B1)
+        gather_piece(2, B1)
+        relu_and_add(A0, 0)
+        relu_and_add(A0, 1)
+        round_pair(2, A2)
+        quantise(A2)
+        project(A2)
         gather_piece(0, B2)
         gather_piece(1, B2)
         relu_and_add(A1, 0)
         relu_and_add(A1, 1)
+        first_relu(1)
         for lo in (0, P):
             round_four(on_scalar, B1, lo, lo + P)
         quantise(B1)
         for jt in range(2):
             relu_and_add(A2, jt)
             project(B1, (2 * jt, 2 * jt + 1))
+        gather_piece(2, B2)
         for lo in (0, P):
-            for i in (2, 3):
-                gather(i, B2 * HALF + lo, B2 * HALF + lo + P)
+            gather(3, B2 * HALF + lo, B2 * HALF + lo + P)
         for lo in (0, P):
             round_four(on_vector, B2, lo, lo + P)
         for lo in (0, P):
             quantise(B2, lo, lo + P)
-        for q in range(2):
-            nc.scalar.activation(pooled_pair(q), banks[2 * pair_of[B0] + q][:], ACT.Relu, bias=zero[:, 0:1])
+        first_relu(0)
         project(B2)
         for nt in range(NT):
             finish(0, nt, banks[2 * sum_pair + nt // 2][:, HALF * (nt % 2) : HALF * (nt % 2 + 1)])

from contextlib import ExitStack

import concourse.mybir as mybir
from concourse.masks import make_identity

K, N, T, J, PICKS = 512, 512, 2048, 512, 3
FLOPS = 2 * K * N * J * PICKS

F32 = mybir.dt.float32
BF16 = mybir.dt.bfloat16
I32 = mybir.dt.int32
U32 = mybir.dt.uint32
U16 = mybir.dt.uint16
U8 = mybir.dt.uint8
FP8X4 = mybir.dt.float8_e4m3fn_x4
FP4X4 = mybir.dt.float4_e2m1fn_x4
ACT = mybir.ActivationFunctionType
ALU = mybir.AluOpType

P = 128
PACK = 4
STRIPE = 16
HALF = 256
NT = N // P
GROUPS = 8
CHUNK = 96
CHUNKS = PICKS * J // CHUNK


def tile_list_relus_silu_kernel(tc, xT, wgt, w_words, w_scales, b, offs, out):
    nc = tc.nc
    with ExitStack() as ctx:
        keep = ctx.enter_context(tc.tile_pool(name="keep", bufs=1))
        psum = ctx.enter_context(tc.psum_pool(name="psum", bufs=1))

        offsets = keep.tile([P, PICKS * J // STRIPE], U16, name="offsets")
        planes = [keep.tile([P, T], F32, name=f"plane{i}") for i in range(PACK)]
        dealt = keep.tile([P, P], F32, name="dealt", align_bytes=64)
        weights = keep.tile([P, PICKS * J], F32, name="weights", align_bytes=64)
        flat = keep.tile([P, 15 * HALF], F32, name="flat")
        w_codes = keep.tile([P, 2 * N], U8, name="w_codes", align_bytes=64)
        w_scale = keep.tile([P, N], U8, name="w_scale", align_bytes=64)
        bias = keep.tile([P, NT], F32, name="bias")
        seed = keep.tile([P, 8], F32, name="seed")
        zero = keep.tile([P, 8], F32, name="zero")
        ident = keep.tile([P, P], F32, name="ident")
        banks = [psum.tile([P, 2 * HALF], F32, name=f"bank{q}") for q in range(8)]

        nc.vector.memset(seed[:], 0.0)
        nc.vector.memset(dealt[:, CHUNK:P], 0.0)
        nc.vector.memset(w_scale[:].bitcast(U32), 0)
        nc.scalar.activation(zero[:], seed[:], ACT.Silu)
        make_identity(nc, ident[:])

        x_planes = xT.rearrange("(p i) t -> i p t", i=PACK)
        nc.sync.dma_start(dealt[:, 0:CHUNK], wgt.rearrange("p (h j) -> (p h) j", h=2)[0 : 2 * P : STRIPE + 1, :])
        nc.sync.dma_start(offsets[:], offs)
        for i in range(PACK):
            nc.sync.dma_start(planes[i][:], x_planes[i])
        nc.sync.dma_start(w_codes[:].bitcast(I32), w_words[0].bitcast(I32))
        for q in range(4):
            nc.sync.dma_start(
                w_scale[32 * q : 32 * q + 4, :].bitcast(I32), w_scales[0, 4 * q : 4 * q + 4, :].bitcast(I32)
            )
        with nc.allow_non_contiguous_dma(reason="one bias value a partition"):
            nc.sync.dma_start(bias[:], b.rearrange("(t p) -> p t", p=P))

        turned = banks[7][:, 0:P]
        nc.tensor.transpose(turned, dealt[:], ident[:])

        on_scalar, on_vector = nc.scalar.copy, nc.vector.tensor_copy
        blocks = keep.tile([P, P], F32, name="blocks", align_bytes=64)
        blocks_repeated = keep.tile([P, 14, 3, 2, STRIPE], F32, name="blocks_repeated", align_bytes=64)
        nc.vector.transpose(blocks[:], dealt[:])
        source = blocks[:, 0:CHUNK].rearrange("p (h g s) -> p s h g", h=3, g=2)
        for copy, lo, hi in ((on_vector, 0, 3), (on_scalar, 3, 8), (on_scalar, 10, 14)):
            copy(blocks_repeated[:, lo:hi], source[:, lo:hi, :, :].unsqueeze(4).to_broadcast([P, hi - lo, 3, 2, STRIPE]))
        for lo, hi in ((0, 256), (256, 768), (1024, 1280)):
            nc.vector.transpose(weights[:, lo:hi], blocks_repeated[:].rearrange("p s h g r -> p (s h g r)")[:, lo:hi])

        early = keep.tile([P, 4, 2, HALF], F32, name="early", align_bytes=64)
        repeated = early[:].rearrange("p n k c -> p (n k) c")[:, :, 0:P]
        for q, first in enumerate((8, 13)):
            source = turned.rearrange("p (g s) -> p s g", g=GROUPS)[:, first : first + 3, :]
            slots = repeated[:, 4 * q : 4 * q + 3, :]
            on_scalar(slots.rearrange("p s (g r) -> p s g r", r=STRIPE), source.unsqueeze(3).to_broadcast([P, 3, GROUPS, STRIPE]))
            for s in range(3):
                nc.tensor.transpose(banks[q][:, CHUNK * s : CHUNK * s + P], slots[:, s, :], ident[:])
            lo = 768 + J * q
            on_scalar(weights[:, lo : lo + HALF], banks[q][:, lo - CHUNK * first : lo - CHUNK * first + HALF])

        late_rows = flat[:].rearrange("p (s j) -> p s j", j=HALF)
        relus = [keep.tile([P, 2, N], F32, name=f"relus{c}", align_bytes=64) for c in range(PICKS)]
        pooled = keep.tile([P, NT, HALF], F32, name="pooled")
        result = [keep.tile([P, NT, HALF], F32, name=f"result{h}") for h in range(2)]
        out_rows = out.rearrange("(t p) j -> p t j", p=P)
        A0, B0, A1, B1, A2, B2 = range(6)
        grouped = {pc: early[:, n].rearrange("p k c -> p (k c)").bitcast(BF16).rearrange("p (j i) -> p j i", i=PACK) for n, pc in enumerate((A0, A1, B0, A2))}
        fifth = keep.tile([P, 2 * HALF], F32, name="fifth", align_bytes=64)
        nc.vector.memset(fifth[:, HALF - 8 : HALF + 8], 0.0)
        grouped[B1] = fifth[:].bitcast(BF16).rearrange("p (j i) -> p j i", i=PACK)
        grouped[B2] = grouped[B1]
        nc.vector.memset(early[:, 3, 1, 1:2], 0.0)
        zero_for = {(A0, 0): early[:, 3, 1, 1:2], (A1, 1): fifth[:, HALF - 1 : HALF], (B0, 1): fifth[:, HALF : HALF + 1]}
        codes = [keep.tile([P, HALF], U32, name=f"codes{pc}", align_bytes=64) for pc in range(6)]
        scales = [keep.tile([P, HALF], U8, name=f"scales{pc}", align_bytes=64) for pc in range(6)]
        rows = {A0: (0, 4, 9, 8), B0: (1, 5, 10, 12), A1: (2, 6, 11, 13), A2: (3, 7, 8, 9), B1: (10, 11, 12, 13), B2: (8, 9, 10, 11)}
        column = {(pc, i): HALF * r for pc in rows for i, r in enumerate(rows[pc])}
        pair_of = {A0: 0, A1: 1, A2: 0, B0: 3, B1: 0}
        last_banks = (2, 3, 6, 7)
        sum_pair = 2

        def gather(i, lo, hi):
            first = column[lo // HALF, i] + lo % HALF
            nc.vector.tensor_tensor(
                flat[:, first : first + hi - lo],
                planes[i][:].indirect(offsets[:, lo // STRIPE : hi // STRIPE]),
                weights[:, lo:hi],
                ALU.mult,
            )

        def gather_piece(i, pc):
            gather(i, pc * HALF, (pc + 1) * HALF)

        def round_pair(i, pc, lo=0, hi=HALF):
            c0, c1 = sorted((column[pc, i], column[pc, i + 1]))
            both = flat[:, c0 : c0 + 2 * (c1 - c0)].rearrange("p (i j) -> p j i", i=2)
            on_scalar(grouped[pc][:, lo:hi, i : i + 2], both[:, lo:hi, :: 1 if c0 == column[pc, i] else -1])

        def round_four(copy, pc, lo, hi):
            r0 = rows[pc][0]
            copy(
                grouped[pc][:, lo:hi, :].rearrange("p (c j) i -> p c i j", j=4),
                late_rows[:, r0 : r0 + PACK, lo:hi].rearrange("p i (c j) -> p c i j", j=4),
            )

        def quantise(pc, lo=0, hi=HALF):
            nc.vector.quantize_mx(
                out=codes[pc][:, lo:hi].bitcast(FP8X4),
                scales=scales[pc][:, lo:hi],
                in_=grouped[pc][:, lo:hi, :].rearrange("p j i -> p (j i)"),
            )

        def product(pc, nt):
            if pc == B2:
                return banks[last_banks[nt]][:, 0:HALF]
            return banks[2 * pair_of[pc] + nt // 2][:, HALF * (nt % 2) : HALF * (nt % 2 + 1)]

        def project(pc, blocks=range(NT)):
            if pc % 2 == 0:
                pair = banks[2 * pair_of[pc] : 2 * pair_of[pc] + 2]
                for jt in range(2):
                    nc.tensor.matmul_mx(
                        out=pair[jt][:],
                        lhsT=codes[pc][:, P * jt : P * (jt + 1)].bitcast(FP8X4),
                        lhsT_scale=scales[pc][:, P * jt : P * (jt + 1)],
                        rhs=w_codes[:].bitcast(FP4X4),
                        rhs_scale=w_scale[:],
                        start=True,
                        stop=True,
                    )
            else:
                for nt in blocks:
                    nc.tensor.matmul_mx(
                        out=product(pc, nt),
                        lhsT=w_codes[:, 2 * P * nt : 2 * P * (nt + 1)].bitcast(FP4X4),
                        lhsT_scale=w_scale[:, P * nt : P * (nt + 1)],
                        rhs=codes[pc][:].bitcast(FP8X4),
                        rhs_scale=scales[pc][:],
                        start=True,
                        stop=True,
                    )

        def relu_and_add(pc, jt):
            c = pc // 2
            nc.scalar.activation(relus[c][:, jt, :], banks[2 * pair_of[pc] + jt][:], ACT.Relu, bias=zero_for.get((pc, jt), zero[:, 0:1]))
            for nt in range(NT):
                col = HALF * (nt % 2) + P * jt
                nc.tensor.matmul(
                    banks[2 * sum_pair + nt // 2][:, col : col + P],
                    relus[c][:, jt, P * nt : P * (nt + 1)],
                    ident[:],
                    start=(c == 0 and col == 0),
                    stop=(c == PICKS - 1 and col == 2 * HALF - P),
                    is_transpose=True,
                )

        def finish(h, nt, source):
            nc.scalar.activation(result[h][:, nt, :], source, ACT.Silu, bias=bias[:, nt : nt + 1])
            cols = slice(h * HALF, (h + 1) * HALF)
            if h == 1 and nt == 3:
                nc.scalar.dma_start(out_rows[:, nt, cols], result[h][:, nt, :])
            elif h == 1 and nt == 2:
                nc.sync.dma_start(out_rows[:, nt, cols], result[h][:, nt, :])
            elif nt % 2 == 1:
                nc.sync.dma_start(out_rows[:, nt - 1 : nt + 1, cols], result[h][:, nt - 1 : nt + 1, :])

        def pooled_pair(q):
            return pooled[:, 2 * q : 2 * q + 2, :].rearrange("p t j -> p (t j)")

        def first_relu(q):
            nc.scalar.activation(pooled_pair(q), banks[2 * pair_of[B0] + q][:], ACT.Relu, bias=zero_for.get((B0, q), zero[:, 0:1]))

        for lo, hi in ((0, 768), (1024, 1280)):
            gather(0, lo, hi)
        for lo, hi in ((0, 256), (256, 768), (1024, 1280)):
            gather(1, lo, hi)
        for pc in (A0, A1, A2, B0):
            round_pair(0, pc)
        gather(2, 0, 3 * HALF)
        for lo in (0, P):
            gather(3, lo, lo + P)
            round_pair(2, A0, lo, lo + P)
        gather_piece(3, A1)
        quantise(A0, 0, P)
        gather_piece(3, B0)
        quantise(A0, P, HALF)
        for pc in (A1, B0):
            round_pair(2, pc)
        project(A0)
        gather_piece(2, A2)
        gather_piece(3, A2)
        quantise(A1)
        project(A1)
        gather_piece(1, B1)
        gather_piece(3, B1)
        quantise(B0)
        project(B0)
        gather_piece(0, B1)
        gather_piece(2, B1)
        relu_and_add(A0, 0)
        relu_and_add(A0, 1)
        round_pair(2, A2)
        quantise(A2)
        project(A2)
        gather_piece(0, B2)
        gather_piece(1, B2)
        relu_and_add(A1, 0)
        relu_and_add(A1, 1)
        first_relu(1)
        for lo in (0, P):
            round_four(on_scalar, B1, lo, lo + P)
        quantise(B1)
        for jt in range(2):
            relu_and_add(A2, jt)
            project(B1, (2 * jt, 2 * jt + 1))
        gather_piece(2, B2)
        for lo in (0, P):
            gather(3, B2 * HALF + lo, B2 * HALF + lo + P)
        for lo in (0, P):
            round_four(on_vector, B2, lo, lo + P)
        for lo in (0, P):
            quantise(B2, lo, lo + P)
        first_relu(0)
        project(B2)
        for nt in range(NT):
            finish(0, nt, banks[2 * sum_pair + nt // 2][:, HALF * (nt % 2) : HALF * (nt % 2 + 1)])
        for q in range(2):
            nc.vector.scalar_tensor_tensor(pooled_pair(q), banks[2 * pair_of[B1] + q][:], 0.0, pooled_pair(q), ALU.max, ALU.add)
        for nt in range(NT):
            part = pooled[:, nt, :]
            source = product(B2, nt)
            nc.vector.scalar_tensor_tensor(part, source, 0.0, part, ALU.max, ALU.add)
            finish(1, nt, part)
